import numpy as np
import ml_dtypes


def mxq(x, axis, fmt="e4m3"):
    dtype, down = {"e4m3": (ml_dtypes.float8_e4m3fn, 7), "e5m2": (ml_dtypes.float8_e5m2, 14)}[fmt]
    v = np.moveaxis(np.asarray(x, np.float32).astype(ml_dtypes.bfloat16).astype(np.float64), axis, -1)
    blocks = v.reshape(v.shape[:-1] + (-1, 32))
    amax = np.abs(blocks).max(-1, keepdims=True)
    byte = np.maximum(np.where(amax > 0, np.frexp(amax)[1] - 1 + 127, 0) - down, 1)
    scale = np.exp2(byte - 127.0)
    codes = (blocks / scale).astype(np.float32).astype(dtype).astype(np.float64)
    return np.moveaxis((codes * scale).reshape(v.shape), -1, axis)


WIDE = False


def mx_kscale(k):
    if not WIDE:
        return np.ones(k)
    levels = np.array([10, -10, 5, -5, 0])
    if k % 512:
        return np.exp2(np.random.permutation(np.resize(levels, k // 32))).repeat(32)
    a = np.empty((k // 512, 16))
    for p in range(k // 512):
        a[p, :8] = np.random.permutation(np.resize(levels, 8))
        for g in range(8):
            far = levels[np.abs(levels - a[p, g]) >= 10]
            a[p, g + 8] = far[np.random.randint(len(far))]
    return np.exp2(a.ravel()).repeat(32)


def f64(x):
    return np.asarray(x).astype(np.float64)


def striped(idx):
    return np.tile(np.asarray(idx).reshape(-1, 16).T, (8, 1)).astype(np.uint16)


def unstriped(offs):
    return offs[:16].T.reshape(-1).astype(np.int64)


E2M1 = np.array([0.0, 0.5, 1.0, 1.5, 2.0, 3.0, 4.0, 6.0, -0.0, -0.5, -1.0, -1.5, -2.0, -3.0, -4.0, -6.0])


def pack_weight(w, fmt):
    k, n = w.shape
    w = f64(np.asarray(w, np.float32).astype(ml_dtypes.bfloat16)).reshape(k // 32, 32, n)
    amax = np.abs(w).max(1)
    if fmt == "e4m3":
        byte = np.frexp(amax)[1] - 1 + 127 - 7
    else:
        mant, ex = np.frexp(amax / 6.0)
        byte = np.where(mant > 0.5, ex, ex - 1) + 127
    byte = np.clip(np.where(amax > 0, byte, 1), 1, 254)
    scaled = (w * np.exp2(127.0 - byte)[:, None, :]).reshape(k, n).astype(np.float32)
    by_word = np.ascontiguousarray(scaled.reshape(k // 512, 128, 4, n).transpose(0, 1, 3, 2))
    if fmt == "e4m3":
        words = by_word.astype(ml_dtypes.float8_e4m3fn).view(np.uint8)
    else:
        c = by_word.astype(ml_dtypes.float4_e2m1fn).view(np.uint8) & 0xF
        words = (c[..., 0::2] | (c[..., 1::2] << 4)).reshape(k // 512, 128, 2 * n)
    return np.ascontiguousarray(words), np.ascontiguousarray(byte.astype(np.uint8).reshape(k // 512, 16, n))


def unpack_weight(words, scales, fmt):
    g, _, n = scales.shape
    words = np.ascontiguousarray(words).reshape(g, 128, n, -1)
    if fmt == "e4m3":
        vals = words.view(ml_dtypes.float8_e4m3fn).astype(np.float64)
    else:
        nib = np.empty((g, 128, n, 4), np.uint8)
        nib[..., 0::2] = words & 0xF
        nib[..., 1::2] = words >> 4
        vals = E2M1[nib]
    vals = vals * np.repeat(np.exp2(scales.astype(np.float64) - 127.0), 8, axis=1)[..., None]
    return vals.transpose(0, 1, 3, 2).reshape(g * 512, n)


K, R, F, T, J, G = 512, 128, 512, 2048, 512, 64


def setup_inputs():
    n = np.random.standard_normal
    idx = np.random.permutation(T)[:J]
    fk = mx_kscale(K)
    dtabp = pack_weight(n((K, T)) / fk[:, None], "e2m1")
    tabp = pack_weight(n((K, T)) / fk[:, None], "e2m1")
    return {
        "dtab_words": dtabp[0],
        "dtab_scales": dtabp[1],
        "tab_words": tabp[0],
        "tab_scales": tabp[1],
        "w1": (n((K, R)) * 1 / np.sqrt(K) * fk[:, None]).astype(np.float32),
        "share": (np.random.uniform(0.3, 1.2, (R, 1))).astype(np.float32),
        "og": (np.random.uniform(0.5, 2.0, (R, 1))).astype(np.float32),
        "base": (0.3 * n((R, G))).astype(np.float32),
        "offs": striped(idx),
    }


def reference(dtab_words, dtab_scales, tab_words, tab_scales, w1, share, og, base, offs):
    idx = unstriped(offs)
    dtabu = unpack_weight(dtab_words, dtab_scales, "e2m1")
    tabu = unpack_weight(tab_words, tab_scales, "e2m1")
    w1q = mxq(f64(w1), 0, "e4m3")
    tabidxg = tabu[:, idx]
    a = w1q.T @ tabidxg
    dtabidxg = dtabu[:, idx]
    ta = w1q.T @ dtabidxg
    m1 = a.reshape(R, G, J // G).mean(axis=2)
    v1 = np.sqrt(np.square(a).reshape(R, G, J // G).mean(axis=2) - np.square(m1) + 0.05)
    u1 = np.tanh(v1 + m1 * f64(share))
    tm1 = ta.reshape(R, G, J // G).mean(axis=2)
    tv1 = ((ta * a * 2.0).reshape(R, G, J // G).mean(axis=2) - tm1 * m1 * 2.0) * 0.5 / v1
    tu1 = (tv1 + tm1 * f64(share)) * (1.0 - np.square(u1))
    y = tu1 * f64(og) + f64(base)
    return y

@@ -1,0 +1,149 @@
+from contextlib import ExitStack
+
+import concourse.mybir as mybir
+
+K, R, T, J, G = 512, 128, 2048, 512, 64
+FLOPS = 2 * 2 * K * R * J
+
+F32 = mybir.dt.float32
+BF16 = mybir.dt.bfloat16
+I32 = mybir.dt.int32
+U32 = mybir.dt.uint32
+U16 = mybir.dt.uint16
+U8 = mybir.dt.uint8
+FP8X4 = mybir.dt.float8_e4m3fn_x4
+FP4X4 = mybir.dt.float4_e2m1fn_x4
+ALU = mybir.AluOpType
+ACT = mybir.ActivationFunctionType
+AX = mybir.AxisListType
+
+P = 128
+GROUP = J // G
+HALVES = 2
+JH = J // HALVES
+GH = G // HALVES
+
+
+def tile_attend_tspreadpool_kernel(tc, dtab_words, dtab_scales, tab_words, tab_scales, w1, share, og, base, offs, out):
+    nc = tc.nc
+    with ExitStack() as ctx:
+        sb = ctx.enter_context(tc.tile_pool(name="sb", bufs=1))
+        ps = ctx.enter_context(tc.psum_pool(name="ps", bufs=1))
+
+        offsets = sb.tile([P, J // 16], U16, name="offsets")
+        nc.sync.dma_start(offsets[:], offs)
+
+        def load_scales(name, src):
+            t = sb.tile([P, T], U8, name=name, align_bytes=64)
+            nc.vector.memset(t[:].bitcast(I32), 0)
+            for f in range(4):
+                nc.sync.dma_start(t[f:P:32, :].bitcast(I32), src[0, f:16:4, :].bitcast(I32))
+            return t
+
+        def load_words(name, src):
+            t = sb.tile([P, T], U16, name=name, align_bytes=64)
+            nc.sync.dma_start(t[:].bitcast(I32), src[0].bitcast(I32))
+            return t
+
+        warm_in = sb.tile([P, 1], F32, name="warm_in")
+        warm_out = sb.tile([P, 1], F32, name="warm_out")
+        nc.gpsimd.memset(warm_in[:], 1.0)
+        nc.scalar.activation(warm_out[:], warm_in[:], ACT.Abs_reciprocal_sqrt)
+
+        w_raw = sb.tile([P, 4, R], F32, name="w_raw")
+        nc.sync.dma_start(w_raw[:], w1.rearrange("(p j) r -> p j r", j=4))
+        ts_win = load_scales("ts_win", tab_scales)
+        tw_win = load_words("tw_win", tab_words)
+        dw_win = load_words("dw_win", dtab_words)
+        ds_win = load_scales("ds_win", dtab_scales)
+        share_t = sb.tile([P, 1], F32, name="share_t", tag="slot_c", align_bytes=64)
+        og_t = sb.tile([P, 1], F32, name="og_t")
+        base_t = sb.tile([P, G], F32, name="base_t")
+        nc.sync.dma_start(share_t[:], share)
+        nc.sync.dma_start(og_t[:], og)
+        nc.sync.dma_start(base_t[:], base)
+
+        w_bf = sb.tile([P, R, 4], BF16, name="w_bf", align_bytes=64)
+        nc.scalar.copy(w_bf[:], w_raw[:].rearrange("p j r -> p r j"))
+        w_codes = sb.tile([P, R], U32, name="w_codes", align_bytes=64)
+        w_scales = sb.tile([P, R], U8, name="w_scales", align_bytes=64)
+
+        def gather(name, win, dtype, h, n, tag):
+            t = sb.tile([P, n], dtype, name=name, tag=tag, align_bytes=64)
+            c = n // 16
+            nc.vector.tensor_copy(t[:], win[:].indirect(offsets[:, h * c:(h + 1) * c]))
+            return t
+
+        def product(name, words, scales):
+            acc = ps.tile([P, JH], F32, name=name)
+            nc.tensor.matmul_mx(out=acc[:], lhsT=w_codes[:].bitcast(FP8X4), lhsT_scale=w_scales[:],
+                                rhs=words.bitcast(FP4X4), rhs_scale=scales, start=True, stop=True)
+            return acc
+
+        def grouped(ap):
+            return ap.rearrange("p (g i) -> p g i", i=GROUP)
+
+        def small(name, tag=None):
+            return sb.tile([P, G], F32, name=name, tag=tag or name, align_bytes=64)
+
+        ts_g = gather("ts_g", ts_win, U8, 0, J, "ts_g")
+        nc.vector.quantize_mx(out=w_codes[:].bitcast(FP8X4), scales=w_scales[:],
+                              in_=w_bf[:].rearrange("p r j -> p (r j)"))
+        a_sb = sb.tile([P, J], F32, name="a_sb")
+        s1, s2 = small("s1"), small("s2")
+        a_ps, sq = [], []
+        for h in range(HALVES):
+            tw_g = gather("tw_g%d" % h, tw_win, U16, h, JH, "tw_g%d" % h)
+            a_ps.append(product("a_ps%d" % h, tw_g[:], ts_g[:, h * JH:(h + 1) * JH]))
+            sq.append(sb.tile([P, JH], F32, name="sq%d" % h))
+            nc.scalar.activation(sq[h][:], a_ps[h][:], ACT.Square)
+        for h in range(HALVES):
+            nc.vector.tensor_reduce(s1[:, h * GH:(h + 1) * GH], grouped(a_ps[h][:]), AX.X, ALU.add)
+            nc.vector.tensor_reduce(s2[:, h * GH:(h + 1) * GH], grouped(sq[h][:]), AX.X, ALU.add)
+            nc.scalar.activation(a_sb[:, h * JH:(h + 1) * JH], a_ps[h][:], ACT.Copy)
+
+        og8 = sb.tile([P, 1], F32, name="og8")
+        og8n = sb.tile([P, 1], F32, name="og8n")
+        nc.gpsimd.tensor_scalar(og8[:], og_t[:], 1.0 / GROUP, 0.0, ALU.mult, ALU.add)
+        nc.gpsimd.tensor_scalar(og8n[:], og_t[:], -1.0 / GROUP, 0.0, ALU.mult, ALU.add)
+
+        msq = small("msq", "slot_a")
+        nc.vector.scalar_tensor_tensor(msq[:], s1[:], -1.0 / GROUP ** 2, s1[:], ALU.mult, ALU.mult)
+        var = small("var")
+        nc.vector.scalar_tensor_tensor(var[:], s2[:], 1.0 / GROUP, msq[:], ALU.mult, ALU.add)
+        mean = small("mean", "slot_b")
+        nc.scalar.activation(mean[:], s1[:], ACT.Copy, scale=1.0 / GROUP)
+        rinv = small("rinv")
+        nc.scalar.activation(rinv[:], var[:], ACT.Abs_reciprocal_sqrt, bias=0.05)
+        dw_g0 = gather("dw_g0", dw_win, U16, 0, JH, "slot_a")
+        v = small("v")
+        nc.vector.scalar_tensor_tensor(v[:], var[:], 0.05, rinv[:], ALU.add, ALU.mult)
+        delta = small("delta")
+        nc.vector.scalar_tensor_tensor(delta[:], v[:], share_t[:], mean[:], ALU.mult, ALU.subtract)
+        z = small("z")
+        nc.vector.scalar_tensor_tensor(z[:], mean[:], share_t[:], v[:], ALU.mult, ALU.add)
+        shifted = sb.tile([P, G, GROUP], F32, name="shifted")
+        nc.gpsimd.tensor_tensor(shifted[:], grouped(a_sb[:]),
+                                delta[:].unsqueeze(2).to_broadcast([P, G, GROUP]), ALU.add)
+        u = small("u")
+        nc.scalar.activation(u[:], z[:], ACT.Tanh)
+        usq = small("usq")
+        nc.scalar.activation(usq[:], u[:], ACT.Square)
+        gain = small("gain")
+        nc.scalar.activation(gain[:], usq[:], ACT.Identity, scale=og8n[:], bias=og8[:])
+        alpha = small("alpha")
+        nc.gpsimd.tensor_tensor(alpha[:], gain[:], rinv[:], ALU.mult)
+
+        ds_g = gather("ds_g", ds_win, U8, 0, J, "slot_b")
+        dw_g1 = gather("dw_g1", dw_win, U16, 1, JH, "slot_c")
+        dot = small("dot")
+        ta_ps = [product("ta_ps%d" % h, w[:], ds_g[:, h * JH:(h + 1) * JH]) for h, w in enumerate((dw_g0, dw_g1))]
+        for h in range(HALVES):
+            prod = sb.tile([P, GH, GROUP], F32, name="prod%d" % h)
+            nc.vector.tensor_tensor(prod[:], grouped(ta_ps[h][:]), shifted[:, h * GH:(h + 1) * GH, :], ALU.mult)
+            nc.vector.tensor_reduce(dot[:, h * GH:(h + 1) * GH], prod[:], AX.X, ALU.add)
+        scaled = small("scaled")
+        nc.vector.tensor_tensor(scaled[:], dot[:], alpha[:], ALU.mult)
+        res = small("res")
+        nc.vector.tensor_tensor(res[:], scaled[:], base_t[:], ALU.add)
+        nc.sync.dma_start(out, res[:])

@@ -22,6 +22,7 @@ GROUP = J // G
 HALVES = 2
 JH = J // HALVES
 GH = G // HALVES
+ROW0 = P - 16
 
 
 def tile_attend_tspreadpool_kernel(tc, dtab_words, dtab_scales, tab_words, tab_scales, w1, share, og, base, offs, out):
@@ -33,11 +34,10 @@ def tile_attend_tspreadpool_kernel(tc, dtab_words, dtab_scales, tab_words, tab_s
         offsets = sb.tile([P, J // 16], U16, name="offsets")
         nc.sync.dma_start(offsets[:], offs)
 
-        def load_scales(name, src):
+        def load_scales(name, src, queue):
             t = sb.tile([P, T], U8, name=name, align_bytes=64)
-            nc.vector.memset(t[:].bitcast(I32), 0)
-            for f in range(4):
-                nc.sync.dma_start(t[f:P:32, :].bitcast(I32), src[0, f:16:4, :].bitcast(I32))
+            queue.dma_start(t[ROW0:P, :].bitcast(I32), src[0].bitcast(I32))
+            nc.vector.memset(t[0:ROW0, :].bitcast(I32), 0)
             return t
 
         def load_words(name, src):
@@ -50,18 +50,18 @@ def tile_attend_tspreadpool_kernel(tc, dtab_words, dtab_scales, tab_words, tab_s
         nc.gpsimd.memset(warm_in[:], 1.0)
         nc.scalar.activation(warm_out[:], warm_in[:], ACT.Abs_reciprocal_sqrt)
 
+        ts_win = load_scales("ts_win", tab_scales, nc.scalar)
+        ds_win = load_scales("ds_win", dtab_scales, nc.sync)
         w_raw = sb.tile([P, 4, R], F32, name="w_raw")
         nc.sync.dma_start(w_raw[:], w1.rearrange("(p j) r -> p j r", j=4))
-        ts_win = load_scales("ts_win", tab_scales)
         tw_win = load_words("tw_win", tab_words)
         dw_win = load_words("dw_win", dtab_words)
-        ds_win = load_scales("ds_win", dtab_scales)
-        share_t = sb.tile([P, 1], F32, name="share_t", tag="slot_c", align_bytes=64)
+        share_t = sb.tile([P, 1], F32, name="share_t")
         og_t = sb.tile([P, 1], F32, name="og_t")
         base_t = sb.tile([P, G], F32, name="base_t")
-        nc.sync.dma_start(share_t[:], share)
-        nc.sync.dma_start(og_t[:], og)
-        nc.sync.dma_start(base_t[:], base)
+        nc.gpsimd.dma_start(share_t[:], share)
+        nc.gpsimd.dma_start(og_t[:], og)
+        nc.gpsimd.dma_start(base_t[:], base)
 
         w_bf = sb.tile([P, R, 4], BF16, name="w_bf", align_bytes=64)
         nc.scalar.copy(w_bf[:], w_raw[:].rearrange("p j r -> p r j"))
@@ -86,10 +86,18 @@ def tile_attend_tspreadpool_kernel(tc, dtab_words, dtab_scales, tab_words, tab_s
         def small(name, tag=None):
             return sb.tile([P, G], F32, name=name, tag=tag or name, align_bytes=64)
 
-        ts_g = gather("ts_g", ts_win, U8, 0, J, "ts_g")
+        def plane(name, win, queues):
+            rows = gather(name + "_rows", win, U8, 0, J, name + "_rows")
+            t = sb.tile([P, J], U8, name=name, align_bytes=64)
+            for f in range(4):
+                queues[f % len(queues)].dma_start(t[f:P:32, :].bitcast(I32), rows[ROW0 + f:P:4, :].bitcast(I32))
+            return t
+
+        ts_g = plane("ts_g", ts_win, (nc.sync, nc.scalar))
+        ds_g = plane("ds_g", ds_win, (nc.sync,))
         nc.vector.quantize_mx(out=w_codes[:].bitcast(FP8X4), scales=w_scales[:],
                               in_=w_bf[:].rearrange("p r j -> p (r j)"))
-        a_sb = sb.tile([P, J], F32, name="a_sb")
+        a_sb = sb.tile([P, JH], F32, name="a_sb")
         s1, s2 = small("s1"), small("s2")
         a_ps, sq = [], []
         for h in range(HALVES):
@@ -97,53 +105,57 @@ def tile_attend_tspreadpool_kernel(tc, dtab_words, dtab_scales, tab_words, tab_s
             a_ps.append(product("a_ps%d" % h, tw_g[:], ts_g[:, h * JH:(h + 1) * JH]))
             sq.append(sb.tile([P, JH], F32, name="sq%d" % h))
             nc.scalar.activation(sq[h][:], a_ps[h][:], ACT.Square)
+        dw_g0 = gather("dw_g0", dw_win, U16, 0, JH, "dw_g0")
         for h in range(HALVES):
             nc.vector.tensor_reduce(s1[:, h * GH:(h + 1) * GH], grouped(a_ps[h][:]), AX.X, ALU.add)
             nc.vector.tensor_reduce(s2[:, h * GH:(h + 1) * GH], grouped(sq[h][:]), AX.X, ALU.add)
-            nc.scalar.activation(a_sb[:, h * JH:(h + 1) * JH], a_ps[h][:], ACT.Copy)
 
-        og8 = sb.tile([P, 1], F32, name="og8")
         og8n = sb.tile([P, 1], F32, name="og8n")
-        nc.gpsimd.tensor_scalar(og8[:], og_t[:], 1.0 / GROUP, 0.0, ALU.mult, ALU.add)
+        share8 = sb.tile([P, 1], F32, name="share8")
+        nc.gpsimd.tensor_scalar(share8[:], share_t[:], 1.0 / GROUP, 0.0, ALU.mult, ALU.add)
         nc.gpsimd.tensor_scalar(og8n[:], og_t[:], -1.0 / GROUP, 0.0, ALU.mult, ALU.add)
 
         msq = small("msq", "slot_a")
-        nc.vector.scalar_tensor_tensor(msq[:], s1[:], -1.0 / GROUP ** 2, s1[:], ALU.mult, ALU.mult)
+        nc.scalar.activation(msq[:], s1[:], ACT.Square, scale=1.0 / GROUP)
+        nc.scalar.activation(a_sb[:], a_ps[1][:], ACT.Copy)
         var = small("var")
-        nc.vector.scalar_tensor_tensor(var[:], s2[:], 1.0 / GROUP, msq[:], ALU.mult, ALU.add)
-        mean = small("mean", "slot_b")
-        nc.scalar.activation(mean[:], s1[:], ACT.Copy, scale=1.0 / GROUP)
+        nc.vector.scalar_tensor_tensor(var[:], s2[:], 1.0 / GROUP, msq[:], ALU.mult, ALU.subtract)
+        mean = small("mean")
+        nc.gpsimd.tensor_scalar(mean[:], s1[:], 1.0 / GROUP, 0.0, ALU.mult, ALU.add)
         rinv = small("rinv")
         nc.scalar.activation(rinv[:], var[:], ACT.Abs_reciprocal_sqrt, bias=0.05)
-        dw_g0 = gather("dw_g0", dw_win, U16, 0, JH, "slot_a")
+        dw_g1 = gather("dw_g1", dw_win, U16, 1, JH, "slot_a")
+        rq = small("rq")
+        nc.gpsimd.tensor_scalar(rq[:], rinv[:], og8n[:], 0.0, ALU.mult, ALU.add)
         v = small("v")
         nc.vector.scalar_tensor_tensor(v[:], var[:], 0.05, rinv[:], ALU.add, ALU.mult)
         delta = small("delta")
         nc.vector.scalar_tensor_tensor(delta[:], v[:], share_t[:], mean[:], ALU.mult, ALU.subtract)
+        shifted = [sb.tile([P, GH, GROUP], F32, name="shifted%d" % h) for h in range(HALVES)]
+        spread = [delta[:, h * GH:(h + 1) * GH].unsqueeze(2).to_broadcast([P, GH, GROUP]) for h in range(HALVES)]
+        nc.gpsimd.tensor_tensor(shifted[1][:], grouped(a_sb[:]), spread[1], ALU.add)
         z = small("z")
-        nc.vector.scalar_tensor_tensor(z[:], mean[:], share_t[:], v[:], ALU.mult, ALU.add)
-        shifted = sb.tile([P, G, GROUP], F32, name="shifted")
-        nc.gpsimd.tensor_tensor(shifted[:], grouped(a_sb[:]),
-                                delta[:].unsqueeze(2).to_broadcast([P, G, GROUP]), ALU.add)
+        nc.vector.scalar_tensor_tensor(z[:], s1[:], share8[:], v[:], ALU.mult, ALU.add)
+        nc.vector.tensor_tensor(shifted[0][:], grouped(a_ps[0][:]), spread[0], ALU.add)
         u = small("u")
         nc.scalar.activation(u[:], z[:], ACT.Tanh)
         usq = small("usq")
         nc.scalar.activation(usq[:], u[:], ACT.Square)
-        gain = small("gain")
-        nc.scalar.activation(gain[:], usq[:], ACT.Identity, scale=og8n[:], bias=og8[:])
-        alpha = small("alpha")
-        nc.gpsimd.tensor_tensor(alpha[:], gain[:], rinv[:], ALU.mult)
 
-        ds_g = gather("ds_g", ds_win, U8, 0, J, "slot_b")
-        dw_g1 = gather("dw_g1", dw_win, U16, 1, JH, "slot_c")
         dot = small("dot")
         ta_ps = [product("ta_ps%d" % h, w[:], ds_g[:, h * JH:(h + 1) * JH]) for h, w in enumerate((dw_g0, dw_g1))]
+        prod = [sb.tile([P, GH, GROUP], F32, name="prod%d" % h) for h in range(HALVES)]
         for h in range(HALVES):
-            prod = sb.tile([P, GH, GROUP], F32, name="prod%d" % h)
-            nc.vector.tensor_tensor(prod[:], grouped(ta_ps[h][:]), shifted[:, h * GH:(h + 1) * GH, :], ALU.mult)
-            nc.vector.tensor_reduce(dot[:, h * GH:(h + 1) * GH], prod[:], AX.X, ALU.add)
+            nc.vector.tensor_tensor(prod[h][:], grouped(ta_ps[h][:]), shifted[h][:], ALU.mult)
+        for h in range(HALVES):
+            nc.vector.tensor_reduce(dot[:, h * GH:(h + 1) * GH], prod[h][:], AX.X, ALU.add)
+        alpha = small("alpha")
+        nc.vector.scalar_tensor_tensor(alpha[:], usq[:], 1.0, rq[:], ALU.subtract, ALU.mult)
         scaled = small("scaled")
-        nc.vector.tensor_tensor(scaled[:], dot[:], alpha[:], ALU.mult)
         res = small("res")
-        nc.vector.tensor_tensor(res[:], scaled[:], base_t[:], ALU.add)
+        cols = [slice(h * GH, (h + 1) * GH) for h in range(HALVES)]
+        for c in cols:
+            nc.vector.tensor_tensor(scaled[:, c], dot[:, c], alpha[:, c], ALU.mult)
+        for c in cols:
+            nc.vector.tensor_tensor(res[:, c], scaled[:, c], base_t[:, c], ALU.add)
         nc.sync.dma_start(out, res[:])

@@ -41,7 +41,7 @@ def tile_attend_tspreadpool_kernel(tc, dtab_words, dtab_scales, tab_words, tab_s
             return t
 
         def load_words(name, src):
-            t = sb.tile([P, T], U16, name=name, align_bytes=64)
+            t = sb.tile([P, T], U16, name=name, tag=name, align_bytes=64)
             nc.sync.dma_start(t[:].bitcast(I32), src[0].bitcast(I32))
             return t
 
@@ -51,11 +51,11 @@ def tile_attend_tspreadpool_kernel(tc, dtab_words, dtab_scales, tab_words, tab_s
         nc.scalar.activation(warm_out[:], warm_in[:], ACT.Abs_reciprocal_sqrt)
 
         ts_win = load_scales("ts_win", tab_scales, nc.scalar)
-        ds_win = load_scales("ds_win", dtab_scales, nc.sync)
+        tw_win = load_words("tw_win", tab_words)
         w_raw = sb.tile([P, 4, R], F32, name="w_raw")
         nc.sync.dma_start(w_raw[:], w1.rearrange("(p j) r -> p j r", j=4))
-        tw_win = load_words("tw_win", tab_words)
         dw_win = load_words("dw_win", dtab_words)
+        ds_win = load_scales("ds_win", dtab_scales, nc.sync)
         share_t = sb.tile([P, 1], F32, name="share_t")
         og_t = sb.tile([P, 1], F32, name="og_t")
         base_t = sb.tile([P, G], F32, name="base_t")
@@ -94,10 +94,8 @@ def tile_attend_tspreadpool_kernel(tc, dtab_words, dtab_scales, tab_words, tab_s
             return t
 
         ts_g = plane("ts_g", ts_win, (nc.sync, nc.scalar))
-        ds_g = plane("ds_g", ds_win, (nc.sync,))
         nc.vector.quantize_mx(out=w_codes[:].bitcast(FP8X4), scales=w_scales[:],
                               in_=w_bf[:].rearrange("p r j -> p (r j)"))
-        a_sb = sb.tile([P, JH], F32, name="a_sb")
         s1, s2 = small("s1"), small("s2")
         a_ps, sq = [], []
         for h in range(HALVES):
@@ -106,6 +104,7 @@ def tile_attend_tspreadpool_kernel(tc, dtab_words, dtab_scales, tab_words, tab_s
             sq.append(sb.tile([P, JH], F32, name="sq%d" % h))
             nc.scalar.activation(sq[h][:], a_ps[h][:], ACT.Square)
         dw_g0 = gather("dw_g0", dw_win, U16, 0, JH, "dw_g0")
+        ds_g = plane("ds_g", ds_win, (nc.sync,))
         for h in range(HALVES):
             nc.vector.tensor_reduce(s1[:, h * GH:(h + 1) * GH], grouped(a_ps[h][:]), AX.X, ALU.add)
             nc.vector.tensor_reduce(s2[:, h * GH:(h + 1) * GH], grouped(sq[h][:]), AX.X, ALU.add)
@@ -115,28 +114,29 @@ def tile_attend_tspreadpool_kernel(tc, dtab_words, dtab_scales, tab_words, tab_s
         nc.gpsimd.tensor_scalar(share8[:], share_t[:], 1.0 / GROUP, 0.0, ALU.mult, ALU.add)
         nc.gpsimd.tensor_scalar(og8n[:], og_t[:], -1.0 / GROUP, 0.0, ALU.mult, ALU.add)
 
-        msq = small("msq", "slot_a")
-        nc.scalar.activation(msq[:], s1[:], ACT.Square, scale=1.0 / GROUP)
-        nc.scalar.activation(a_sb[:], a_ps[1][:], ACT.Copy)
+        msq = small("msq")
+        inv64 = sb.tile([P, 1], F32, name="inv64", tag="slot_a", align_bytes=64)
+        nc.gpsimd.memset(inv64[:], 1.0 / GROUP ** 2)
+        nc.vector.scalar_tensor_tensor(msq[:], s1[:], inv64[:], s1[:], ALU.mult, ALU.mult)
         var = small("var")
         nc.vector.scalar_tensor_tensor(var[:], s2[:], 1.0 / GROUP, msq[:], ALU.mult, ALU.subtract)
         mean = small("mean")
-        nc.gpsimd.tensor_scalar(mean[:], s1[:], 1.0 / GROUP, 0.0, ALU.mult, ALU.add)
+        nc.scalar.activation(mean[:], s1[:], ACT.Copy, scale=1.0 / GROUP)
         rinv = small("rinv")
         nc.scalar.activation(rinv[:], var[:], ACT.Abs_reciprocal_sqrt, bias=0.05)
         dw_g1 = gather("dw_g1", dw_win, U16, 1, JH, "slot_a")
-        rq = small("rq")
-        nc.gpsimd.tensor_scalar(rq[:], rinv[:], og8n[:], 0.0, ALU.mult, ALU.add)
         v = small("v")
         nc.vector.scalar_tensor_tensor(v[:], var[:], 0.05, rinv[:], ALU.add, ALU.mult)
+        rq = small("rq", "slot_r")
+        nc.vector.tensor_scalar(rq[:], rinv[:], og8n[:], None, ALU.mult)
         delta = small("delta")
         nc.vector.scalar_tensor_tensor(delta[:], v[:], share_t[:], mean[:], ALU.mult, ALU.subtract)
         shifted = [sb.tile([P, GH, GROUP], F32, name="shifted%d" % h) for h in range(HALVES)]
         spread = [delta[:, h * GH:(h + 1) * GH].unsqueeze(2).to_broadcast([P, GH, GROUP]) for h in range(HALVES)]
-        nc.gpsimd.tensor_tensor(shifted[1][:], grouped(a_sb[:]), spread[1], ALU.add)
         z = small("z")
         nc.vector.scalar_tensor_tensor(z[:], s1[:], share8[:], v[:], ALU.mult, ALU.add)
-        nc.vector.tensor_tensor(shifted[0][:], grouped(a_ps[0][:]), spread[0], ALU.add)
+        for h in range(HALVES):
+            nc.vector.tensor_tensor(shifted[h][:], grouped(a_ps[h][:]), spread[h], ALU.add)
         u = small("u")
         nc.scalar.activation(u[:], z[:], ACT.Tanh)
         usq = small("usq")

from contextlib import ExitStack

import concourse.mybir as mybir

K, R, T, J, G = 512, 128, 2048, 512, 64
FLOPS = 2 * 2 * K * R * J

F32 = mybir.dt.float32
BF16 = mybir.dt.bfloat16
I32 = mybir.dt.int32
U32 = mybir.dt.uint32
U16 = mybir.dt.uint16
U8 = mybir.dt.uint8
FP8X4 = mybir.dt.float8_e4m3fn_x4
FP4X4 = mybir.dt.float4_e2m1fn_x4
ALU = mybir.AluOpType
ACT = mybir.ActivationFunctionType
AX = mybir.AxisListType

P = 128
GROUP = J // G
HALVES = 2
JH = J // HALVES
GH = G // HALVES
ROW0 = P - 16


def tile_attend_tspreadpool_kernel(tc, dtab_words, dtab_scales, tab_words, tab_scales, w1, share, og, base, offs, out):
    nc = tc.nc
    with ExitStack() as ctx:
        sb = ctx.enter_context(tc.tile_pool(name="sb", bufs=1))
        ps = ctx.enter_context(tc.psum_pool(name="ps", bufs=1))

        offsets = sb.tile([P, J // 16], U16, name="offsets")
        nc.sync.dma_start(offsets[:], offs)

        def load_scales(name, src, queue):
            t = sb.tile([P, T], U8, name=name, align_bytes=64)
            queue.dma_start(t[ROW0:P, :].bitcast(I32), src[0].bitcast(I32))
            nc.vector.memset(t[0:ROW0, :].bitcast(I32), 0)
            return t

        def load_words(name, src):
            t = sb.tile([P, T], U16, name=name, tag=name, align_bytes=64)
            nc.sync.dma_start(t[:].bitcast(I32), src[0].bitcast(I32))
            return t

        warm_in = sb.tile([P, 1], F32, name="warm_in")
        warm_out = sb.tile([P, 1], F32, name="warm_out")
        nc.gpsimd.memset(warm_in[:], 1.0)
        nc.scalar.activation(warm_out[:], warm_in[:], ACT.Abs_reciprocal_sqrt)

        ts_win = load_scales("ts_win", tab_scales, nc.scalar)
        tw_win = load_words("tw_win", tab_words)
        w_raw = sb.tile([P, 4, R], F32, name="w_raw")
        nc.sync.dma_start(w_raw[:], w1.rearrange("(p j) r -> p j r", j=4))
        dw_win = load_words("dw_win", dtab_words)
        ds_win = load_scales("ds_win", dtab_scales, nc.sync)
        share_t = sb.tile([P, 1], F32, name="share_t")
        og_t = sb.tile([P, 1], F32, name="og_t")
        base_t = sb.tile([P, G], F32, name="base_t")
        nc.gpsimd.dma_start(share_t[:], share)
        nc.gpsimd.dma_start(og_t[:], og)
        nc.gpsimd.dma_start(base_t[:], base)

        w_bf = sb.tile([P, R, 4], BF16, name="w_bf", align_bytes=64)
        nc.scalar.copy(w_bf[:], w_raw[:].rearrange("p j r -> p r j"))
        w_codes = sb.tile([P, R], U32, name="w_codes", align_bytes=64)
        w_scales = sb.tile([P, R], U8, name="w_scales", align_bytes=64)

        def gather(name, win, dtype, h, n, tag):
            t = sb.tile([P, n], dtype, name=name, tag=tag, align_bytes=64)
            c = n // 16
            nc.vector.tensor_copy(t[:], win[:].indirect(offsets[:, h * c:(h + 1) * c]))
            return t

        def product(name, words, scales):
            acc = ps.tile([P, JH], F32, name=name)
            nc.tensor.matmul_mx(out=acc[:], lhsT=w_codes[:].bitcast(FP8X4), lhsT_scale=w_scales[:],
                                rhs=words.bitcast(FP4X4), rhs_scale=scales, start=True, stop=True)
            return acc

        def grouped(ap):
            return ap.rearrange("p (g i) -> p g i", i=GROUP)

        def small(name, tag=None):
            return sb.tile([P, G], F32, name=name, tag=tag or name, align_bytes=64)

        def plane(name, win, queues):
            rows = gather(name + "_rows", win, U8, 0, J, name + "_rows")
            t = sb.tile([P, J], U8, name=name, align_bytes=64)
            for f in range(4):
                queues[f % len(queues)].dma_start(t[f:P:32, :].bitcast(I32), rows[ROW0 + f:P:4, :].bitcast(I32))
            return t

        ts_g = plane("ts_g", ts_win, (nc.sync, nc.scalar))
        nc.vector.quantize_mx(out=w_codes[:].bitcast(FP8X4), scales=w_scales[:],
                              in_=w_bf[:].rearrange("p r j -> p (r j)"))
        s1, s2 = small("s1"), small("s2")
        a_ps, sq = [], []
        for h in range(HALVES):
            tw_g = gather("tw_g%d" % h, tw_win, U16, h, JH, "tw_g%d" % h)
            a_ps.append(product("a_ps%d" % h, tw_g[:], ts_g[:, h * JH:(h + 1) * JH]))
            sq.append(sb.tile([P, JH], F32, name="sq%d" % h))
            nc.scalar.activation(sq[h][:], a_ps[h][:], ACT.Square)
        dw_g0 = gather("dw_g0", dw_win, U16, 0, JH, "dw_g0")
        ds_g = plane("ds_g", ds_win, (nc.sync,))
        for h in range(HALVES):
            nc.vector.tensor_reduce(s1[:, h * GH:(h + 1) * GH], grouped(a_ps[h][:]), AX.X, ALU.add)
            nc.vector.tensor_reduce(s2[:, h * GH:(h + 1) * GH], grouped(sq[h][:]), AX.X, ALU.add)

        og8n = sb.tile([P, 1], F32, name="og8n")
        share8 = sb.tile([P, 1], F32, name="share8")
        nc.gpsimd.tensor_scalar(share8[:], share_t[:], 1.0 / GROUP, 0.0, ALU.mult, ALU.add)
        nc.gpsimd.tensor_scalar(og8n[:], og_t[:], -1.0 / GROUP, 0.0, ALU.mult, ALU.add)

        msq = small("msq")
        inv64 = sb.tile([P, 1], F32, name="inv64", tag="slot_a", align_bytes=64)
        nc.gpsimd.memset(inv64[:], 1.0 / GROUP ** 2)
        nc.vector.scalar_tensor_tensor(msq[:], s1[:], inv64[:], s1[:], ALU.mult, ALU.mult)
        var = small("var")
        nc.vector.scalar_tensor_tensor(var[:], s2[:], 1.0 / GROUP, msq[:], ALU.mult, ALU.subtract)
        mean = small("mean")
        nc.scalar.activation(mean[:], s1[:], ACT.Copy, scale=1.0 / GROUP)
        rinv = small("rinv")
        nc.scalar.activation(rinv[:], var[:], ACT.Abs_reciprocal_sqrt, bias=0.05)
        dw_g1 = gather("dw_g1", dw_win, U16, 1, JH, "slot_a")
        v = small("v")
        nc.vector.scalar_tensor_tensor(v[:], var[:], 0.05, rinv[:], ALU.add, ALU.mult)
        rq = small("rq", "slot_r")
        nc.vector.tensor_scalar(rq[:], rinv[:], og8n[:], None, ALU.mult)
        delta = small("delta")
        nc.vector.scalar_tensor_tensor(delta[:], v[:], share_t[:], mean[:], ALU.mult, ALU.subtract)
        shifted = [sb.tile([P, GH, GROUP], F32, name="shifted%d" % h) for h in range(HALVES)]
        spread = [delta[:, h * GH:(h + 1) * GH].unsqueeze(2).to_broadcast([P, GH, GROUP]) for h in range(HALVES)]
        z = small("z")
        nc.vector.scalar_tensor_tensor(z[:], s1[:], share8[:], v[:], ALU.mult, ALU.add)
        for h in range(HALVES):
            nc.vector.tensor_tensor(shifted[h][:], grouped(a_ps[h][:]), spread[h], ALU.add)
        u = small("u")
        nc.scalar.activation(u[:], z[:], ACT.Tanh)
        usq = small("usq")
        nc.scalar.activation(usq[:], u[:], ACT.Square)

        dot = small("dot")
        ta_ps = [product("ta_ps%d" % h, w[:], ds_g[:, h * JH:(h + 1) * JH]) for h, w in enumerate((dw_g0, dw_g1))]
        prod = [sb.tile([P, GH, GROUP], F32, name="prod%d" % h) for h in range(HALVES)]
        for h in range(HALVES):
            nc.vector.tensor_tensor(prod[h][:], grouped(ta_ps[h][:]), shifted[h][:], ALU.mult)
        for h in range(HALVES):
            nc.vector.tensor_reduce(dot[:, h * GH:(h + 1) * GH], prod[h][:], AX.X, ALU.add)
        alpha = small("alpha")
        nc.vector.scalar_tensor_tensor(alpha[:], usq[:], 1.0, rq[:], ALU.subtract, ALU.mult)
        scaled = small("scaled")
        res = small("res")
        cols = [slice(h * GH, (h + 1) * GH) for h in range(HALVES)]
        for c in cols:
            nc.vector.tensor_tensor(scaled[:, c], dot[:, c], alpha[:, c], ALU.mult)
        for c in cols:
            nc.vector.tensor_tensor(res[:, c], scaled[:, c], base_t[:, c], ALU.add)
        nc.sync.dma_start(out, res[:])
